import numpy as np, ml_dtypes
CORES = [0,1,2,3,4,5,6,7]
N = 8
ROOT = 7
def setup_inputs(rng):
    return {"x": rng.standard_normal((N, 128, N * 2048), dtype=np.float32).astype(ml_dtypes.bfloat16)}
def reference(x):
    return {"y": np.stack([x[ROOT][:, r * 2048:(r + 1) * 2048] for r in range(N)])}

BLK = 2048
NBLK = 8

SCRATCH = {
    "stage": ("sbuf", [128, (NBLK - 1) * BLK], "bfloat16"),
    "land": ("sbuf", [128, BLK], "bfloat16"),
}
SEMAPHORES = ["ld0", "ld1", "ld2", "ld3", "ld4", "ld5", "ld6", "own", "sent", "arrived", "stored"]


def rank_program(g, core, T, topo):
    rank = T.rank_of(core)
    if rank is None:
        return

    root_rank = T.root if T.root is not None else NBLK - 1
    root_core = T.cores[root_rank]

    if core != root_core:
        g.sync.wait_ge(T.sem.arrived, 16)
        g.sync.dma_start(T.y[:, :], T.land[:, :]).then_inc(T.sem.stored, 16)
        g.sync.wait_ge(T.sem.stored, 16)
        return

    others = [r for r in range(NBLK) if r != root_rank]

    g.dma_start(T.y[:, :], T.x[:, root_rank * BLK:(root_rank + 1) * BLK]).then_inc(T.sem.own, 16)

    for k, r in enumerate(others):
        q = g.sync if k % 2 == 0 else g.scalar
        q.dma_start(T.stage[:, k * BLK:(k + 1) * BLK], T.x[:, r * BLK:(r + 1) * BLK]).then_inc(T.sem["ld%d" % k], 16)

    for k, r in enumerate(others):
        dst = T.cores[r]
        rid, pid, _se = topo.addr(dst)
        g.wait_ge(T.sem["ld%d" % k], 16)
        g.remote_dma(T.land[:, :], T.stage[:, k * BLK:(k + 1) * BLK], T.sem.arrived, T.sem.sent,
                     pid, rid, topo.mask(core, dst))

    g.wait_ge(T.sem.sent, 16 * len(others))
    g.wait_ge(T.sem.own, 16)
